import numpy as np
import ml_dtypes


def mxq(x, axis, fmt="e4m3"):
    dtype, down = {"e4m3": (ml_dtypes.float8_e4m3fn, 7), "e5m2": (ml_dtypes.float8_e5m2, 14)}[fmt]
    v = np.moveaxis(np.asarray(x, np.float32).astype(ml_dtypes.bfloat16).astype(np.float64), axis, -1)
    blocks = v.reshape(v.shape[:-1] + (-1, 32))
    amax = np.abs(blocks).max(-1, keepdims=True)
    byte = np.maximum(np.where(amax > 0, np.frexp(amax)[1] - 1 + 127, 0) - down, 1)
    scale = np.exp2(byte - 127.0)
    codes = (blocks / scale).astype(np.float32).astype(dtype).astype(np.float64)
    return np.moveaxis((codes * scale).reshape(v.shape), -1, axis)


WIDE = False


def mx_kscale(k):
    if not WIDE:
        return np.ones(k)
    levels = np.array([10, -10, 5, -5, 0])
    if k % 512:
        return np.exp2(np.random.permutation(np.resize(levels, k // 32))).repeat(32)
    a = np.empty((k // 512, 16))
    for p in range(k // 512):
        a[p, :8] = np.random.permutation(np.resize(levels, 8))
        for g in range(8):
            far = levels[np.abs(levels - a[p, g]) >= 10]
            a[p, g + 8] = far[np.random.randint(len(far))]
    return np.exp2(a.ravel()).repeat(32)


def f64(x):
    return np.asarray(x).astype(np.float64)


def striped(idx):
    return np.tile(np.asarray(idx).reshape(-1, 16).T, (8, 1)).astype(np.uint16)


def unstriped(offs):
    return offs[:16].T.reshape(-1).astype(np.int64)


E2M1 = np.array([0.0, 0.5, 1.0, 1.5, 2.0, 3.0, 4.0, 6.0, -0.0, -0.5, -1.0, -1.5, -2.0, -3.0, -4.0, -6.0])


def pack_weight(w, fmt):
    k, n = w.shape
    w = f64(np.asarray(w, np.float32).astype(ml_dtypes.bfloat16)).reshape(k // 32, 32, n)
    amax = np.abs(w).max(1)
    if fmt == "e4m3":
        byte = np.frexp(amax)[1] - 1 + 127 - 7
    else:
        mant, ex = np.frexp(amax / 6.0)
        byte = np.where(mant > 0.5, ex, ex - 1) + 127
    byte = np.clip(np.where(amax > 0, byte, 1), 1, 254)
    scaled = (w * np.exp2(127.0 - byte)[:, None, :]).reshape(k, n).astype(np.float32)
    by_word = np.ascontiguousarray(scaled.reshape(k // 512, 128, 4, n).transpose(0, 1, 3, 2))
    if fmt == "e4m3":
        words = by_word.astype(ml_dtypes.float8_e4m3fn).view(np.uint8)
    else:
        c = by_word.astype(ml_dtypes.float4_e2m1fn).view(np.uint8) & 0xF
        words = (c[..., 0::2] | (c[..., 1::2] << 4)).reshape(k // 512, 128, 2 * n)
    return np.ascontiguousarray(words), np.ascontiguousarray(byte.astype(np.uint8).reshape(k // 512, 16, n))


def unpack_weight(words, scales, fmt):
    g, _, n = scales.shape
    words = np.ascontiguousarray(words).reshape(g, 128, n, -1)
    if fmt == "e4m3":
        vals = words.view(ml_dtypes.float8_e4m3fn).astype(np.float64)
    else:
        nib = np.empty((g, 128, n, 4), np.uint8)
        nib[..., 0::2] = words & 0xF
        nib[..., 1::2] = words >> 4
        vals = E2M1[nib]
    vals = vals * np.repeat(np.exp2(scales.astype(np.float64) - 127.0), 8, axis=1)[..., None]
    return vals.transpose(0, 1, 3, 2).reshape(g * 512, n)


D, E, T, I, Q = 512, 512, 2048, 512, 128


def setup_inputs():
    n = np.random.standard_normal
    idx = np.random.permutation(T)[:I]
    fd = mx_kscale(D)
    fe = mx_kscale(E)
    keysp = pack_weight(n((D, T)) / fd[:, None], "e4m3")
    valsp = pack_weight(n((E, T)) / fe[:, None], "e4m3")
    return {
        "query": (n((D, Q)) * 0.6 / np.sqrt(D) * fd[:, None]).astype(np.float32),
        "keys_words": keysp[0],
        "keys_scales": keysp[1],
        "pen": (np.random.uniform(0.2, 0.8, (Q, 1))).astype(np.float32),
        "gout": (n((E, Q)) * 1 / np.sqrt(E) * fe[:, None]).astype(np.float32),
        "vals_words": valsp[0],
        "vals_scales": valsp[1],
        "old": (0.5 * n((Q, T))).astype(np.float32),
        "offs": striped(idx),
    }


def reference(query, keys_words, keys_scales, pen, gout, vals_words, vals_scales, old, offs):
    idx = unstriped(offs)
    keysu = unpack_weight(keys_words, keys_scales, "e4m3")
    valsu = unpack_weight(vals_words, vals_scales, "e4m3")
    queryq = mxq(f64(query), 0, "e4m3")
    keysidxg = keysu[:, idx]
    a = queryq.T @ keysidxg
    p = np.exp(a - np.max(a, axis=1, keepdims=True))
    z = np.sum(p, axis=1, keepdims=True)
    goutq = mxq(f64(gout), 0, "e4m3")
    valsidxg = valsu[:, idx]
    c0 = goutq.T @ valsidxg
    m1 = np.sum(p * c0, axis=1, keepdims=True) / z
    dm1 = 1.0 + f64(pen) * m1 * 2.0
    dz = f64(pen) * (-1.0) * np.sum(p * np.square(c0), axis=1, keepdims=True) / np.square(z) * (-1.0) - dm1 * np.sum(p * c0, axis=1, keepdims=True) / np.square(z)
    dp = f64(pen) * (-1.0) / z * np.square(c0) + dm1 / z * c0 + dz
    da = dp * p
    gs = da * 512.0
    gf = np.zeros((Q, T))
    gf[:, idx] = gs
    y = f64(old) + gf
    return y

@@ -1,0 +1,154 @@
+from contextlib import ExitStack
+
+import concourse.mybir as mybir
+
+D, T, I, Q = 512, 2048, 512, 128
+FLOPS = 2 * 2 * D * I * Q
+
+F32 = mybir.dt.float32
+BF16 = mybir.dt.bfloat16
+I32 = mybir.dt.int32
+U32 = mybir.dt.uint32
+U16 = mybir.dt.uint16
+U8 = mybir.dt.uint8
+FP8X4 = mybir.dt.float8_e4m3fn_x4
+ALU = mybir.AluOpType
+ACT = mybir.ActivationFunctionType
+AX = mybir.AxisListType
+
+P = 128
+PACK = 4
+HALF = I // 2
+VAL_ROW = 4
+STORE_WIDTHS = (512, 512, 512, 512)
+
+
+def load_scale_rows(queues, plane, scales, first_row):
+    for quad, queue in enumerate(queues):
+        lo = 32 * quad + first_row
+        queue.dma_start(out=plane[lo : lo + 4, :].bitcast(I32), in_=scales[0, 4 * quad : 4 * quad + 4, :].bitcast(I32))
+
+
+def interleave(nc, grouped, raw):
+    nc.scalar.copy(
+        out=grouped[:].rearrange("p (c i) t -> p c t i", i=4),
+        in_=raw[:].rearrange("p t (c i) -> p c t i", i=4),
+    )
+
+
+def tile_attend_bspreadpenalty_s_kernel(tc, query, keys_words, keys_scales, pen, gout, vals_words, vals_scales, old, offs, out):
+    nc = tc.nc
+    with ExitStack() as ctx:
+        sb = ctx.enter_context(tc.tile_pool(name="sb", bufs=1))
+        ps = ctx.enter_context(tc.psum_pool(name="ps", bufs=1))
+
+        offsets = sb.tile([P, I // 16], U16, name="offsets")
+        nc.sync.dma_start(offsets[:], offs)
+
+        key_plane = sb.tile([P, T], U8, name="key_plane")
+        val_plane = sb.tile([P, T], U8, name="val_plane")
+        window = sb.tile([P, T], F32, name="window")
+        warm_in = sb.tile([P, 1], F32, name="warm_in")
+        warm_out = sb.tile([P, 1], F32, name="warm_out")
+        nc.vector.memset(key_plane[:].bitcast(I32), 0)
+        nc.vector.memset(warm_in[:], 0.0)
+        nc.vector.memset(val_plane[:].bitcast(I32), 0)
+        for lo in range(0, T, 512):
+            nc.vector.memset(window[:, lo : lo + 512], 0.0)
+
+        q_raw = sb.tile([P, PACK, Q], F32, name="q_raw", tag="raw")
+        nc.sync.dma_start(out=q_raw[:], in_=query.rearrange("(p t) q -> p t q", t=PACK))
+        key_pool = sb.tile([P, T], I32, name="key_pool", tag="big", align_bytes=64)
+        nc.sync.dma_start(out=key_pool[:], in_=keys_words[0].rearrange("p n t -> p (n t)").bitcast(I32))
+        val_pool = sb.tile([P, T], I32, name="val_pool")
+        nc.sync.dma_start(out=val_pool[:], in_=vals_words[0].rearrange("p n t -> p (n t)").bitcast(I32))
+        load_scale_rows([nc.scalar] * 4, key_plane, keys_scales, 0)
+        load_scale_rows([nc.scalar, nc.scalar, nc.gpsimd, nc.gpsimd], val_plane, vals_scales, VAL_ROW)
+        nc.scalar.activation(out=warm_out[:], in_=warm_in[:], func=ACT.Exp)
+        pen_col = sb.tile([P, 1], F32, name="pen_col")
+        nc.gpsimd.dma_start(out=pen_col[:], in_=pen)
+
+        key_scale = sb.tile([P, I], U8, name="key_scale", align_bytes=64)
+        nc.vector.tensor_copy(key_scale[:], key_plane[:].indirect(offsets[:]))
+
+        q_bf = sb.tile([P, Q, PACK], BF16, name="q_bf", align_bytes=64)
+        interleave(nc, q_bf, q_raw)
+        g_raw = sb.tile([P, PACK, Q], F32, name="g_raw", tag="raw")
+        nc.scalar.dma_start(out=g_raw[:], in_=gout.rearrange("(p t) q -> p t q", t=PACK))
+        q_codes = sb.tile([P, Q], U32, name="q_codes", align_bytes=64)
+        q_scale = sb.tile([P, Q], U8, name="q_scale", align_bytes=64)
+        nc.vector.quantize_mx(out=q_codes[:].bitcast(FP8X4), scales=q_scale[:], in_=q_bf[:].rearrange("p q t -> p (q t)"))
+
+        key_codes = sb.tile([P, I], U32, name="key_codes", align_bytes=64)
+        nc.vector.tensor_copy(key_codes[:], key_pool[:].bitcast(U32).indirect(offsets[:]))
+
+        a_ps = ps.tile([P, I], F32, name="a_ps")
+        nc.tensor.matmul_mx(out=a_ps[:], lhsT=q_codes[:].bitcast(FP8X4), lhsT_scale=q_scale[:],
+                            rhs=key_codes[:].bitcast(FP8X4), rhs_scale=key_scale[:], start=True, stop=True)
+
+        val_scale = sb.tile([P, I], U8, name="val_scale", tag="big", align_bytes=64)
+        nc.vector.tensor_copy(val_scale[:], val_plane[:].indirect(offsets[:]))
+
+        neg_max = sb.tile([P, 1], F32, name="neg_max")
+        neg_a = sb.tile([P, I], F32, name="neg_a", tag="val_codes0", align_bytes=64)
+        nc.vector.tensor_scalar(neg_a[:], a_ps[:], -1.0, None, ALU.mult, ALU.min, accum_out=neg_max[:])
+        p = sb.tile([P, I], F32, name="p")
+        z = sb.tile([P, 1], F32, name="z")
+        nc.scalar.activation(out=p[:], in_=a_ps[:], func=ACT.Exp, bias=neg_max[:], accum_out=z[:])
+
+        g_bf = sb.tile([P, Q, PACK], BF16, name="g_bf", align_bytes=64)
+        interleave(nc, g_bf, g_raw)
+        old_sb = sb.tile([P, T], F32, name="old_sb", tag="raw")
+        nc.sync.dma_start(out=old_sb[:], in_=old)
+        g_codes = sb.tile([P, Q], U32, name="g_codes", align_bytes=64)
+        g_scale = sb.tile([P, Q], U8, name="g_scale", align_bytes=64)
+        nc.vector.quantize_mx(out=g_codes[:].bitcast(FP8X4), scales=g_scale[:], in_=g_bf[:].rearrange("p q t -> p (q t)"))
+
+        slope = sb.tile([P, 1], F32, name="slope")
+        mean_gain = sb.tile([P, 1], F32, name="mean_gain")
+        nc.scalar.mul(slope[:], pen_col[:], -512.0)
+        nc.scalar.mul(mean_gain[:], pen_col[:], 1024.0)
+
+        c_ps = []
+        for h in range(2):
+            codes = sb.tile([P, HALF], U32, name=f"val_codes{h}", tag=f"val_codes{h}", align_bytes=64)
+            nc.vector.tensor_copy(codes[:], val_pool[:].bitcast(U32).indirect(offsets[:, h * HALF // 16 : (h + 1) * HALF // 16]))
+            bank = ps.tile([P, HALF], F32, name=f"c_ps{h}")
+            nc.tensor.matmul_mx(out=bank[:], lhsT=g_codes[:].bitcast(FP8X4), lhsT_scale=g_scale[:],
+                                rhs=codes[:].bitcast(FP8X4), rhs_scale=val_scale[VAL_ROW:P, h * HALF : (h + 1) * HALF],
+                                start=True, stop=True)
+            c_ps.append(bank)
+
+        rz = sb.tile([P, 1], F32, name="rz")
+        neg_rz = sb.tile([P, 1], F32, name="neg_rz")
+        nc.vector.reciprocal(rz[:], z[:])
+        nc.scalar.mul(neg_rz[:], rz[:], -1.0)
+
+        line = sb.tile([P, I], F32, name="line")
+        pc = sb.tile([P, I], F32, name="pc")
+        means = []
+        for h in range(2):
+            cols = slice(h * HALF, (h + 1) * HALF)
+            nc.scalar.activation(out=line[:, cols], in_=c_ps[h][:], func=ACT.Copy, scale=slope[:], bias=512.0)
+            mean = sb.tile([P, 1], F32, name=f"mean{h}")
+            nc.vector.scalar_tensor_tensor(out=pc[:, cols], in0=c_ps[h][:], scalar=rz[:], in1=p[:, cols],
+                                           op0=ALU.mult, op1=ALU.mult, accum_out=mean[:])
+            means.append(mean)
+        shift = sb.tile([P, 1], F32, name="shift")
+        nc.vector.tensor_scalar(shift[:], means[0][:], means[1][:], mean_gain[:], ALU.add, ALU.mult)
+        w = sb.tile([P, I], F32, name="w")
+        w_sum = sb.tile([P, 1], F32, name="w_sum")
+        nc.vector.scalar_tensor_tensor(out=w[:], in0=line[:], scalar=shift[:], in1=pc[:],
+                                       op0=ALU.add, op1=ALU.mult, accum_out=w_sum[:])
+        centre = sb.tile([P, I], F32, name="centre")
+        nc.vector.tensor_scalar(centre[:], p[:], w_sum[:], neg_rz[:], ALU.mult, ALU.mult)
+        nc.vector.tensor_tensor(window[:].indirect(offsets[:]), w[:], centre[:], ALU.add)
+
+        lo = 0
+        for n, width in enumerate(STORE_WIDTHS):
+            cols = slice(lo, lo + width)
+            res = sb.tile([P, width], F32, name=f"res{n}")
+            nc.vector.tensor_tensor(res[:], old_sb[:, cols], window[:, cols], ALU.add)
+            queue = nc.sync if n % 2 == 0 else nc.scalar
+            queue.dma_start(out=out[:, cols], in_=res[:])
+            lo += width

@@ -20,7 +20,7 @@ P = 128
 PACK = 4
 HALF = I // 2
 VAL_ROW = 4
-STORE_WIDTHS = (512, 512, 512, 512)
+STORE_WIDTHS = (256, 512, 512, 512, 256)
 
 
 def load_scale_rows(queues, plane, scales, first_row):
@@ -45,64 +45,66 @@ def tile_attend_bspreadpenalty_s_kernel(tc, query, keys_words, keys_scales, pen,
         offsets = sb.tile([P, I // 16], U16, name="offsets")
         nc.sync.dma_start(offsets[:], offs)
 
-        key_plane = sb.tile([P, T], U8, name="key_plane")
-        val_plane = sb.tile([P, T], U8, name="val_plane")
-        window = sb.tile([P, T], F32, name="window")
-        warm_in = sb.tile([P, 1], F32, name="warm_in")
-        warm_out = sb.tile([P, 1], F32, name="warm_out")
-        nc.vector.memset(key_plane[:].bitcast(I32), 0)
-        nc.vector.memset(warm_in[:], 0.0)
-        nc.vector.memset(val_plane[:].bitcast(I32), 0)
-        for lo in range(0, T, 512):
-            nc.vector.memset(window[:, lo : lo + 512], 0.0)
-
-        q_raw = sb.tile([P, PACK, Q], F32, name="q_raw", tag="raw")
+        q_raw = sb.tile([P, PACK, Q], F32, name="q_raw", tag="q_then_pen")
         nc.sync.dma_start(out=q_raw[:], in_=query.rearrange("(p t) q -> p t q", t=PACK))
+        g_raw = sb.tile([P, PACK, Q], F32, name="g_raw", tag="g_then_vals")
+        nc.sync.dma_start(out=g_raw[:], in_=gout.rearrange("(p t) q -> p t q", t=PACK))
+
+        warm_in = sb.tile([P, 1], F32, name="warm_in", tag="big", align_bytes=64)
+        warm_out = sb.tile([P, 1], F32, name="warm_out", tag="val_plane", align_bytes=64)
+        key_plane = sb.tile([P, T], U8, name="key_plane")
+        window = sb.tile([P, T], F32, name="window")
+        nc.vector.memset(warm_in[:], 0.0)
+        nc.vector.memset(key_plane[:].bitcast(I32), 0)
+        nc.scalar.activation(out=warm_out[:], in_=warm_in[:], func=ACT.Exp)
+        load_scale_rows([nc.sync] * 4, key_plane, keys_scales, 0)
+        nc.vector.memset(window[:, : T // 2], 0.0)
+
         key_pool = sb.tile([P, T], I32, name="key_pool", tag="big", align_bytes=64)
         nc.sync.dma_start(out=key_pool[:], in_=keys_words[0].rearrange("p n t -> p (n t)").bitcast(I32))
-        val_pool = sb.tile([P, T], I32, name="val_pool")
-        nc.sync.dma_start(out=val_pool[:], in_=vals_words[0].rearrange("p n t -> p (n t)").bitcast(I32))
-        load_scale_rows([nc.scalar] * 4, key_plane, keys_scales, 0)
-        load_scale_rows([nc.scalar, nc.scalar, nc.gpsimd, nc.gpsimd], val_plane, vals_scales, VAL_ROW)
-        nc.scalar.activation(out=warm_out[:], in_=warm_in[:], func=ACT.Exp)
-        pen_col = sb.tile([P, 1], F32, name="pen_col")
-        nc.gpsimd.dma_start(out=pen_col[:], in_=pen)
+        val_plane = sb.tile([P, T], U8, name="val_plane", tag="val_plane", align_bytes=64)
+        nc.vector.memset(val_plane[:].bitcast(I32), 0)
+        load_scale_rows([nc.sync] * 4, val_plane, vals_scales, VAL_ROW)
+        nc.vector.memset(window[:, T // 2 :], 0.0)
 
         key_scale = sb.tile([P, I], U8, name="key_scale", align_bytes=64)
         nc.vector.tensor_copy(key_scale[:], key_plane[:].indirect(offsets[:]))
 
         q_bf = sb.tile([P, Q, PACK], BF16, name="q_bf", align_bytes=64)
         interleave(nc, q_bf, q_raw)
-        g_raw = sb.tile([P, PACK, Q], F32, name="g_raw", tag="raw")
-        nc.scalar.dma_start(out=g_raw[:], in_=gout.rearrange("(p t) q -> p t q", t=PACK))
+        pen_col = sb.tile([P, 1], F32, name="pen_col", tag="q_then_pen")
+        nc.sync.dma_start(out=pen_col[:], in_=pen)
         q_codes = sb.tile([P, Q], U32, name="q_codes", align_bytes=64)
         q_scale = sb.tile([P, Q], U8, name="q_scale", align_bytes=64)
         nc.vector.quantize_mx(out=q_codes[:].bitcast(FP8X4), scales=q_scale[:], in_=q_bf[:].rearrange("p q t -> p (q t)"))
 
-        key_codes = sb.tile([P, I], U32, name="key_codes", align_bytes=64)
+        g_bf = sb.tile([P, Q, PACK], BF16, name="g_bf", align_bytes=64)
+        interleave(nc, g_bf, g_raw)
+        val_pool = sb.tile([P, T], I32, name="val_pool", tag="g_then_vals")
+        nc.sync.dma_start(out=val_pool[:], in_=vals_words[0].rearrange("p n t -> p (n t)").bitcast(I32))
+        g_codes = sb.tile([P, Q], U32, name="g_codes", align_bytes=64)
+        g_scale = sb.tile([P, Q], U8, name="g_scale", align_bytes=64)
+        nc.vector.quantize_mx(out=g_codes[:].bitcast(FP8X4), scales=g_scale[:], in_=g_bf[:].rearrange("p q t -> p (q t)"))
+
+        key_codes = sb.tile([P, I], U32, name="key_codes", tag="keys_then_old", align_bytes=64)
         nc.vector.tensor_copy(key_codes[:], key_pool[:].bitcast(U32).indirect(offsets[:]))
 
         a_ps = ps.tile([P, I], F32, name="a_ps")
         nc.tensor.matmul_mx(out=a_ps[:], lhsT=q_codes[:].bitcast(FP8X4), lhsT_scale=q_scale[:],
                             rhs=key_codes[:].bitcast(FP8X4), rhs_scale=key_scale[:], start=True, stop=True)
 
+        old_sb = sb.tile([P, T], F32, name="old_sb", tag="keys_then_old", align_bytes=64)
+        nc.sync.dma_start(out=old_sb[:], in_=old)
+
         val_scale = sb.tile([P, I], U8, name="val_scale", tag="big", align_bytes=64)
         nc.vector.tensor_copy(val_scale[:], val_plane[:].indirect(offsets[:]))
 
         neg_max = sb.tile([P, 1], F32, name="neg_max")
-        neg_a = sb.tile([P, I], F32, name="neg_a", tag="val_codes0", align_bytes=64)
+        neg_a = sb.tile([P, I], F32, name="neg_a", tag="val_plane", align_bytes=64)
         nc.vector.tensor_scalar(neg_a[:], a_ps[:], -1.0, None, ALU.mult, ALU.min, accum_out=neg_max[:])
         p = sb.tile([P, I], F32, name="p")
         z = sb.tile([P, 1], F32, name="z")
         nc.scalar.activation(out=p[:], in_=a_ps[:], func=ACT.Exp, bias=neg_max[:], accum_out=z[:])
-
-        g_bf = sb.tile([P, Q, PACK], BF16, name="g_bf", align_bytes=64)
-        interleave(nc, g_bf, g_raw)
-        old_sb = sb.tile([P, T], F32, name="old_sb", tag="raw")
-        nc.sync.dma_start(out=old_sb[:], in_=old)
-        g_codes = sb.tile([P, Q], U32, name="g_codes", align_bytes=64)
-        g_scale = sb.tile([P, Q], U8, name="g_scale", align_bytes=64)
-        nc.vector.quantize_mx(out=g_codes[:].bitcast(FP8X4), scales=g_scale[:], in_=g_bf[:].rearrange("p q t -> p (q t)"))
 
         slope = sb.tile([P, 1], F32, name="slope")
         mean_gain = sb.tile([P, 1], F32, name="mean_gain")
@@ -110,12 +112,13 @@ def tile_attend_bspreadpenalty_s_kernel(tc, query, keys_words, keys_scales, pen,
         nc.scalar.mul(mean_gain[:], pen_col[:], 1024.0)
 
         c_ps = []
+        val_codes = sb.tile([P, I], U32, name="val_codes", tag="val_plane", align_bytes=64)
         for h in range(2):
-            codes = sb.tile([P, HALF], U32, name=f"val_codes{h}", tag=f"val_codes{h}", align_bytes=64)
-            nc.vector.tensor_copy(codes[:], val_pool[:].bitcast(U32).indirect(offsets[:, h * HALF // 16 : (h + 1) * HALF // 16]))
+            codes = val_codes[:, h * HALF : (h + 1) * HALF]
+            nc.vector.tensor_copy(codes, val_pool[:].bitcast(U32).indirect(offsets[:, h * HALF // 16 : (h + 1) * HALF // 16]))
             bank = ps.tile([P, HALF], F32, name=f"c_ps{h}")
             nc.tensor.matmul_mx(out=bank[:], lhsT=g_codes[:].bitcast(FP8X4), lhsT_scale=g_scale[:],
-                                rhs=codes[:].bitcast(FP8X4), rhs_scale=val_scale[VAL_ROW:P, h * HALF : (h + 1) * HALF],
+                                rhs=codes.bitcast(FP8X4), rhs_scale=val_scale[VAL_ROW:P, h * HALF : (h + 1) * HALF],
                                 start=True, stop=True)
             c_ps.append(bank)
 
@@ -129,10 +132,10 @@ def tile_attend_bspreadpenalty_s_kernel(tc, query, keys_words, keys_scales, pen,
         means = []
         for h in range(2):
             cols = slice(h * HALF, (h + 1) * HALF)
-            nc.scalar.activation(out=line[:, cols], in_=c_ps[h][:], func=ACT.Copy, scale=slope[:], bias=512.0)
             mean = sb.tile([P, 1], F32, name=f"mean{h}")
             nc.vector.scalar_tensor_tensor(out=pc[:, cols], in0=c_ps[h][:], scalar=rz[:], in1=p[:, cols],
                                            op0=ALU.mult, op1=ALU.mult, accum_out=mean[:])
+            nc.scalar.activation(out=line[:, cols], in_=c_ps[h][:], func=ACT.Copy, scale=slope[:], bias=512.0)
             means.append(mean)
         shift = sb.tile([P, 1], F32, name="shift")
         nc.vector.tensor_scalar(shift[:], means[0][:], means[1][:], mean_gain[:], ALU.add, ALU.mult)

@@ -23,15 +23,14 @@ VAL_ROW = 4
 STORE_WIDTHS = (256, 512, 512, 512, 256)
 
 
-def load_scale_rows(queues, plane, scales, first_row):
-    for quad, queue in enumerate(queues):
-        lo = 32 * quad + first_row
-        queue.dma_start(out=plane[lo : lo + 4, :].bitcast(I32), in_=scales[0, 4 * quad : 4 * quad + 4, :].bitcast(I32))
+def load_scale_rows(nc, plane, scales, first_row):
+    for r in range(4):
+        nc.sync.dma_start(out=plane[first_row + r : P : 32, :].bitcast(I32), in_=scales[0, r : 16 : 4, :].bitcast(I32))
 
 
 def interleave(nc, grouped, raw):
     nc.scalar.copy(
-        out=grouped[:].rearrange("p (c i) t -> p c t i", i=4),
+        out=grouped.rearrange("p (c i) t -> p c t i", i=4),
         in_=raw[:].rearrange("p t (c i) -> p c t i", i=4),
     )
 
@@ -45,58 +44,52 @@ def tile_attend_bspreadpenalty_s_kernel(tc, query, keys_words, keys_scales, pen,
         offsets = sb.tile([P, I // 16], U16, name="offsets")
         nc.sync.dma_start(offsets[:], offs)
 
+        key_plane = sb.tile([P, T], U8, name="key_plane", tag="key_plane", align_bytes=64)
+        nc.vector.memset(key_plane[:, :1280].bitcast(I32), 0)
+        nc.gpsimd.memset(key_plane[:, 1280:].bitcast(I32), 0)
         q_raw = sb.tile([P, PACK, Q], F32, name="q_raw", tag="q_then_pen")
         nc.sync.dma_start(out=q_raw[:], in_=query.rearrange("(p t) q -> p t q", t=PACK))
-        g_raw = sb.tile([P, PACK, Q], F32, name="g_raw", tag="g_then_vals")
+        g_raw = sb.tile([P, PACK, Q], F32, name="g_raw")
         nc.sync.dma_start(out=g_raw[:], in_=gout.rearrange("(p t) q -> p t q", t=PACK))
+        load_scale_rows(nc, key_plane, keys_scales, 0)
+        key_pool = sb.tile([P, T], I32, name="key_pool")
+        nc.sync.dma_start(out=key_pool[:], in_=keys_words[0].rearrange("p n t -> p (n t)").bitcast(I32))
 
-        warm_in = sb.tile([P, 1], F32, name="warm_in", tag="big", align_bytes=64)
-        warm_out = sb.tile([P, 1], F32, name="warm_out", tag="val_plane", align_bytes=64)
-        key_plane = sb.tile([P, T], U8, name="key_plane")
+        warm_in = sb.tile([P, 1], F32, name="warm_in", tag="warm_then_vals")
+        warm_out = sb.tile([P, 1], F32, name="warm_out")
         window = sb.tile([P, T], F32, name="window")
         nc.vector.memset(warm_in[:], 0.0)
-        nc.vector.memset(key_plane[:].bitcast(I32), 0)
         nc.scalar.activation(out=warm_out[:], in_=warm_in[:], func=ACT.Exp)
-        load_scale_rows([nc.sync] * 4, key_plane, keys_scales, 0)
-        nc.vector.memset(window[:, : T // 2], 0.0)
-
-        key_pool = sb.tile([P, T], I32, name="key_pool", tag="big", align_bytes=64)
-        nc.sync.dma_start(out=key_pool[:], in_=keys_words[0].rearrange("p n t -> p (n t)").bitcast(I32))
         val_plane = sb.tile([P, T], U8, name="val_plane", tag="val_plane", align_bytes=64)
         nc.vector.memset(val_plane[:].bitcast(I32), 0)
-        load_scale_rows([nc.sync] * 4, val_plane, vals_scales, VAL_ROW)
-        nc.vector.memset(window[:, T // 2 :], 0.0)
+        load_scale_rows(nc, val_plane, vals_scales, VAL_ROW)
+        nc.vector.memset(window[:], 0.0)
+        val_pool = sb.tile([P, T], I32, name="val_pool", tag="warm_then_vals")
+        nc.sync.dma_start(out=val_pool[:], in_=vals_words[0].rearrange("p n t -> p (n t)").bitcast(I32))
 
-        key_scale = sb.tile([P, I], U8, name="key_scale", align_bytes=64)
+        key_scale = sb.tile([P, I], U8, name="key_scale", tag="key_scale", align_bytes=64)
         nc.vector.tensor_copy(key_scale[:], key_plane[:].indirect(offsets[:]))
 
-        q_bf = sb.tile([P, Q, PACK], BF16, name="q_bf", align_bytes=64)
-        interleave(nc, q_bf, q_raw)
+        rows_bf = sb.tile([P, 2, Q, PACK], BF16, name="rows_bf", align_bytes=64)
+        interleave(nc, rows_bf[:, 0], q_raw)
         pen_col = sb.tile([P, 1], F32, name="pen_col", tag="q_then_pen")
-        nc.sync.dma_start(out=pen_col[:], in_=pen)
-        q_codes = sb.tile([P, Q], U32, name="q_codes", align_bytes=64)
-        q_scale = sb.tile([P, Q], U8, name="q_scale", align_bytes=64)
-        nc.vector.quantize_mx(out=q_codes[:].bitcast(FP8X4), scales=q_scale[:], in_=q_bf[:].rearrange("p q t -> p (q t)"))
+        nc.scalar.dma_start(out=pen_col[:], in_=pen)
+        interleave(nc, rows_bf[:, 1], g_raw)
+        row_codes = sb.tile([P, 2 * Q], U32, name="row_codes", align_bytes=64)
+        row_scale = sb.tile([P, 2 * Q], U8, name="row_scale", tag="key_plane", align_bytes=64)
+        nc.vector.quantize_mx(out=row_codes[:].bitcast(FP8X4), scales=row_scale[:], in_=rows_bf[:].rearrange("p s q t -> p (s q t)"))
 
-        g_bf = sb.tile([P, Q, PACK], BF16, name="g_bf", align_bytes=64)
-        interleave(nc, g_bf, g_raw)
-        val_pool = sb.tile([P, T], I32, name="val_pool", tag="g_then_vals")
-        nc.sync.dma_start(out=val_pool[:], in_=vals_words[0].rearrange("p n t -> p (n t)").bitcast(I32))
-        g_codes = sb.tile([P, Q], U32, name="g_codes", align_bytes=64)
-        g_scale = sb.tile([P, Q], U8, name="g_scale", align_bytes=64)
-        nc.vector.quantize_mx(out=g_codes[:].bitcast(FP8X4), scales=g_scale[:], in_=g_bf[:].rearrange("p q t -> p (q t)"))
-
-        key_codes = sb.tile([P, I], U32, name="key_codes", tag="keys_then_old", align_bytes=64)
+        key_codes = sb.tile([P, I], U32, name="key_codes", tag="codes", align_bytes=64)
         nc.vector.tensor_copy(key_codes[:], key_pool[:].bitcast(U32).indirect(offsets[:]))
 
         a_ps = ps.tile([P, I], F32, name="a_ps")
-        nc.tensor.matmul_mx(out=a_ps[:], lhsT=q_codes[:].bitcast(FP8X4), lhsT_scale=q_scale[:],
+        nc.tensor.matmul_mx(out=a_ps[:], lhsT=row_codes[:, :Q].bitcast(FP8X4), lhsT_scale=row_scale[:, :Q],
                             rhs=key_codes[:].bitcast(FP8X4), rhs_scale=key_scale[:], start=True, stop=True)
 
-        old_sb = sb.tile([P, T], F32, name="old_sb", tag="keys_then_old", align_bytes=64)
+        old_sb = sb.tile([P, T], F32, name="old_sb", tag="key_scale", align_bytes=64)
         nc.sync.dma_start(out=old_sb[:], in_=old)
 
-        val_scale = sb.tile([P, I], U8, name="val_scale", tag="big", align_bytes=64)
+        val_scale = sb.tile([P, I], U8, name="val_scale", align_bytes=64)
         nc.vector.tensor_copy(val_scale[:], val_plane[:].indirect(offsets[:]))
 
         neg_max = sb.tile([P, 1], F32, name="neg_max")
@@ -112,17 +105,17 @@ def tile_attend_bspreadpenalty_s_kernel(tc, query, keys_words, keys_scales, pen,
         nc.scalar.mul(mean_gain[:], pen_col[:], 1024.0)
 
         c_ps = []
-        val_codes = sb.tile([P, I], U32, name="val_codes", tag="val_plane", align_bytes=64)
+        val_codes = sb.tile([P, I], U32, name="val_codes", tag="codes", align_bytes=64)
         for h in range(2):
             codes = val_codes[:, h * HALF : (h + 1) * HALF]
             nc.vector.tensor_copy(codes, val_pool[:].bitcast(U32).indirect(offsets[:, h * HALF // 16 : (h + 1) * HALF // 16]))
             bank = ps.tile([P, HALF], F32, name=f"c_ps{h}")
-            nc.tensor.matmul_mx(out=bank[:], lhsT=g_codes[:].bitcast(FP8X4), lhsT_scale=g_scale[:],
+            nc.tensor.matmul_mx(out=bank[:], lhsT=row_codes[:, Q:].bitcast(FP8X4), lhsT_scale=row_scale[:, Q:],
                                 rhs=codes.bitcast(FP8X4), rhs_scale=val_scale[VAL_ROW:P, h * HALF : (h + 1) * HALF],
                                 start=True, stop=True)
             c_ps.append(bank)
 
-        rz = sb.tile([P, 1], F32, name="rz")
+        rz = sb.tile([P, 1], F32, name="rz", tag="warm_then_vals")
         neg_rz = sb.tile([P, 1], F32, name="neg_rz")
         nc.vector.reciprocal(rz[:], z[:])
         nc.scalar.mul(neg_rz[:], rz[:], -1.0)
@@ -130,13 +123,14 @@ def tile_attend_bspreadpenalty_s_kernel(tc, query, keys_words, keys_scales, pen,
         line = sb.tile([P, I], F32, name="line")
         pc = sb.tile([P, I], F32, name="pc")
         means = []
+        nc.scalar.activation(out=line[:, :HALF], in_=c_ps[0][:], func=ACT.Copy, scale=slope[:], bias=512.0)
         for h in range(2):
             cols = slice(h * HALF, (h + 1) * HALF)
             mean = sb.tile([P, 1], F32, name=f"mean{h}")
             nc.vector.scalar_tensor_tensor(out=pc[:, cols], in0=c_ps[h][:], scalar=rz[:], in1=p[:, cols],
                                            op0=ALU.mult, op1=ALU.mult, accum_out=mean[:])
-            nc.scalar.activation(out=line[:, cols], in_=c_ps[h][:], func=ACT.Copy, scale=slope[:], bias=512.0)
             means.append(mean)
+        nc.scalar.activation(out=line[:, HALF:], in_=c_ps[1][:], func=ACT.Copy, scale=slope[:], bias=512.0)
         shift = sb.tile([P, 1], F32, name="shift")
         nc.vector.tensor_scalar(shift[:], means[0][:], means[1][:], mean_gain[:], ALU.add, ALU.mult)
         w = sb.tile([P, I], F32, name="w")

@@ -56,13 +56,13 @@ def tile_attend_bspreadpenalty_s_kernel(tc, query, keys_words, keys_scales, pen,
         nc.sync.dma_start(out=key_pool[:], in_=keys_words[0].rearrange("p n t -> p (n t)").bitcast(I32))
 
         warm_in = sb.tile([P, 1], F32, name="warm_in", tag="warm_then_vals")
-        warm_out = sb.tile([P, 1], F32, name="warm_out")
-        window = sb.tile([P, T], F32, name="window")
+        warm_out = sb.tile([P, 1], F32, name="warm_out", tag="warm_then_window")
         nc.vector.memset(warm_in[:], 0.0)
         nc.scalar.activation(out=warm_out[:], in_=warm_in[:], func=ACT.Exp)
         val_plane = sb.tile([P, T], U8, name="val_plane", tag="val_plane", align_bytes=64)
         nc.vector.memset(val_plane[:].bitcast(I32), 0)
         load_scale_rows(nc, val_plane, vals_scales, VAL_ROW)
+        window = sb.tile([P, T], F32, name="window", tag="warm_then_window")
         nc.vector.memset(window[:], 0.0)
         val_pool = sb.tile([P, T], I32, name="val_pool", tag="warm_then_vals")
         nc.sync.dma_start(out=val_pool[:], in_=vals_words[0].rearrange("p n t -> p (n t)").bitcast(I32))

from contextlib import ExitStack

import concourse.mybir as mybir

D, T, I, Q = 512, 2048, 512, 128
FLOPS = 2 * 2 * D * I * Q

F32 = mybir.dt.float32
BF16 = mybir.dt.bfloat16
I32 = mybir.dt.int32
U32 = mybir.dt.uint32
U16 = mybir.dt.uint16
U8 = mybir.dt.uint8
FP8X4 = mybir.dt.float8_e4m3fn_x4
ALU = mybir.AluOpType
ACT = mybir.ActivationFunctionType
AX = mybir.AxisListType

P = 128
PACK = 4
HALF = I // 2
VAL_ROW = 4
STORE_WIDTHS = (256, 512, 512, 512, 256)


def load_scale_rows(nc, plane, scales, first_row):
    for r in range(4):
        nc.sync.dma_start(out=plane[first_row + r : P : 32, :].bitcast(I32), in_=scales[0, r : 16 : 4, :].bitcast(I32))


def interleave(nc, grouped, raw):
    nc.scalar.copy(
        out=grouped.rearrange("p (c i) t -> p c t i", i=4),
        in_=raw[:].rearrange("p t (c i) -> p c t i", i=4),
    )


def tile_attend_bspreadpenalty_s_kernel(tc, query, keys_words, keys_scales, pen, gout, vals_words, vals_scales, old, offs, out):
    nc = tc.nc
    with ExitStack() as ctx:
        sb = ctx.enter_context(tc.tile_pool(name="sb", bufs=1))
        ps = ctx.enter_context(tc.psum_pool(name="ps", bufs=1))

        offsets = sb.tile([P, I // 16], U16, name="offsets")
        nc.sync.dma_start(offsets[:], offs)

        key_plane = sb.tile([P, T], U8, name="key_plane", tag="key_plane", align_bytes=64)
        nc.vector.memset(key_plane[:, :1280].bitcast(I32), 0)
        nc.gpsimd.memset(key_plane[:, 1280:].bitcast(I32), 0)
        q_raw = sb.tile([P, PACK, Q], F32, name="q_raw", tag="q_then_pen")
        nc.sync.dma_start(out=q_raw[:], in_=query.rearrange("(p t) q -> p t q", t=PACK))
        g_raw = sb.tile([P, PACK, Q], F32, name="g_raw")
        nc.sync.dma_start(out=g_raw[:], in_=gout.rearrange("(p t) q -> p t q", t=PACK))
        load_scale_rows(nc, key_plane, keys_scales, 0)
        key_pool = sb.tile([P, T], I32, name="key_pool")
        nc.sync.dma_start(out=key_pool[:], in_=keys_words[0].rearrange("p n t -> p (n t)").bitcast(I32))

        warm_in = sb.tile([P, 1], F32, name="warm_in", tag="warm_then_vals")
        warm_out = sb.tile([P, 1], F32, name="warm_out", tag="warm_then_window")
        nc.vector.memset(warm_in[:], 0.0)
        nc.scalar.activation(out=warm_out[:], in_=warm_in[:], func=ACT.Exp)
        val_plane = sb.tile([P, T], U8, name="val_plane", tag="val_plane", align_bytes=64)
        nc.vector.memset(val_plane[:].bitcast(I32), 0)
        load_scale_rows(nc, val_plane, vals_scales, VAL_ROW)
        window = sb.tile([P, T], F32, name="window", tag="warm_then_window")
        nc.vector.memset(window[:], 0.0)
        val_pool = sb.tile([P, T], I32, name="val_pool", tag="warm_then_vals")
        nc.sync.dma_start(out=val_pool[:], in_=vals_words[0].rearrange("p n t -> p (n t)").bitcast(I32))

        key_scale = sb.tile([P, I], U8, name="key_scale", tag="key_scale", align_bytes=64)
        nc.vector.tensor_copy(key_scale[:], key_plane[:].indirect(offsets[:]))

        rows_bf = sb.tile([P, 2, Q, PACK], BF16, name="rows_bf", align_bytes=64)
        interleave(nc, rows_bf[:, 0], q_raw)
        pen_col = sb.tile([P, 1], F32, name="pen_col", tag="q_then_pen")
        nc.scalar.dma_start(out=pen_col[:], in_=pen)
        interleave(nc, rows_bf[:, 1], g_raw)
        row_codes = sb.tile([P, 2 * Q], U32, name="row_codes", align_bytes=64)
        row_scale = sb.tile([P, 2 * Q], U8, name="row_scale", tag="key_plane", align_bytes=64)
        nc.vector.quantize_mx(out=row_codes[:].bitcast(FP8X4), scales=row_scale[:], in_=rows_bf[:].rearrange("p s q t -> p (s q t)"))

        key_codes = sb.tile([P, I], U32, name="key_codes", tag="codes", align_bytes=64)
        nc.vector.tensor_copy(key_codes[:], key_pool[:].bitcast(U32).indirect(offsets[:]))

        a_ps = ps.tile([P, I], F32, name="a_ps")
        nc.tensor.matmul_mx(out=a_ps[:], lhsT=row_codes[:, :Q].bitcast(FP8X4), lhsT_scale=row_scale[:, :Q],
                            rhs=key_codes[:].bitcast(FP8X4), rhs_scale=key_scale[:], start=True, stop=True)

        old_sb = sb.tile([P, T], F32, name="old_sb", tag="key_scale", align_bytes=64)
        nc.sync.dma_start(out=old_sb[:], in_=old)

        val_scale = sb.tile([P, I], U8, name="val_scale", align_bytes=64)
        nc.vector.tensor_copy(val_scale[:], val_plane[:].indirect(offsets[:]))

        neg_max = sb.tile([P, 1], F32, name="neg_max")
        neg_a = sb.tile([P, I], F32, name="neg_a", tag="val_plane", align_bytes=64)
        nc.vector.tensor_scalar(neg_a[:], a_ps[:], -1.0, None, ALU.mult, ALU.min, accum_out=neg_max[:])
        p = sb.tile([P, I], F32, name="p")
        z = sb.tile([P, 1], F32, name="z")
        nc.scalar.activation(out=p[:], in_=a_ps[:], func=ACT.Exp, bias=neg_max[:], accum_out=z[:])

        slope = sb.tile([P, 1], F32, name="slope")
        mean_gain = sb.tile([P, 1], F32, name="mean_gain")
        nc.scalar.mul(slope[:], pen_col[:], -512.0)
        nc.scalar.mul(mean_gain[:], pen_col[:], 1024.0)

        c_ps = []
        val_codes = sb.tile([P, I], U32, name="val_codes", tag="codes", align_bytes=64)
        for h in range(2):
            codes = val_codes[:, h * HALF : (h + 1) * HALF]
            nc.vector.tensor_copy(codes, val_pool[:].bitcast(U32).indirect(offsets[:, h * HALF // 16 : (h + 1) * HALF // 16]))
            bank = ps.tile([P, HALF], F32, name=f"c_ps{h}")
            nc.tensor.matmul_mx(out=bank[:], lhsT=row_codes[:, Q:].bitcast(FP8X4), lhsT_scale=row_scale[:, Q:],
                                rhs=codes.bitcast(FP8X4), rhs_scale=val_scale[VAL_ROW:P, h * HALF : (h + 1) * HALF],
                                start=True, stop=True)
            c_ps.append(bank)

        rz = sb.tile([P, 1], F32, name="rz", tag="warm_then_vals")
        neg_rz = sb.tile([P, 1], F32, name="neg_rz")
        nc.vector.reciprocal(rz[:], z[:])
        nc.scalar.mul(neg_rz[:], rz[:], -1.0)

        line = sb.tile([P, I], F32, name="line")
        pc = sb.tile([P, I], F32, name="pc")
        means = []
        nc.scalar.activation(out=line[:, :HALF], in_=c_ps[0][:], func=ACT.Copy, scale=slope[:], bias=512.0)
        for h in range(2):
            cols = slice(h * HALF, (h + 1) * HALF)
            mean = sb.tile([P, 1], F32, name=f"mean{h}")
            nc.vector.scalar_tensor_tensor(out=pc[:, cols], in0=c_ps[h][:], scalar=rz[:], in1=p[:, cols],
                                           op0=ALU.mult, op1=ALU.mult, accum_out=mean[:])
            means.append(mean)
        nc.scalar.activation(out=line[:, HALF:], in_=c_ps[1][:], func=ACT.Copy, scale=slope[:], bias=512.0)
        shift = sb.tile([P, 1], F32, name="shift")
        nc.vector.tensor_scalar(shift[:], means[0][:], means[1][:], mean_gain[:], ALU.add, ALU.mult)
        w = sb.tile([P, I], F32, name="w")
        w_sum = sb.tile([P, 1], F32, name="w_sum")
        nc.vector.scalar_tensor_tensor(out=w[:], in0=line[:], scalar=shift[:], in1=pc[:],
                                       op0=ALU.add, op1=ALU.mult, accum_out=w_sum[:])
        centre = sb.tile([P, I], F32, name="centre")
        nc.vector.tensor_scalar(centre[:], p[:], w_sum[:], neg_rz[:], ALU.mult, ALU.mult)
        nc.vector.tensor_tensor(window[:].indirect(offsets[:]), w[:], centre[:], ALU.add)

        lo = 0
        for n, width in enumerate(STORE_WIDTHS):
            cols = slice(lo, lo + width)
            res = sb.tile([P, width], F32, name=f"res{n}")
            nc.vector.tensor_tensor(res[:], old_sb[:, cols], window[:, cols], ALU.add)
            queue = nc.sync if n % 2 == 0 else nc.scalar
            queue.dma_start(out=out[:, cols], in_=res[:])
            lo += width
